import numpy as np, ml_dtypes
CORES = [9,17,57,81,121,137,145,185,209,249]
N = 10
TK, NT = 256, 5
def setup_inputs(rng):
    x = rng.standard_normal((NT, 128, TK), dtype=np.float32).astype(ml_dtypes.bfloat16)
    return {"x": np.broadcast_to(x, (2, NT, 128, TK)).reshape(N, 128, TK).copy(), "w": rng.standard_normal((N, 128, NT * 128), dtype=np.float32).astype(ml_dtypes.bfloat16)}
def setup_inputs_big(rng):
    d = setup_inputs(rng)
    for k in ("x", "w"): d[k] = (d[k].astype(np.float32) * 1024.0).astype(d[k].dtype)
    return d
def setup_inputs_small(rng):
    d = setup_inputs(rng)
    for k in ("x", "w"): d[k] = (d[k].astype(np.float32) * (1 / 1024.0)).astype(d[k].dtype)
    return d
def setup_inputs_apart(rng):
    d = setup_inputs(rng)
    f = (10.0 ** rng.permutation(np.linspace(-1.5, 1.5, N))).astype(np.float32).reshape(N, 1, 1)
    for k in ("x", "w"): d[k] = (d[k].astype(np.float32) * f).astype(d[k].dtype)
    return d
def tie_inputs(x):
    x = dict(x)
    x["x"] = np.concatenate([x["x"][:NT], x["x"][:NT]])
    return x
def reference(x, w):
    X, W = x.astype(np.float64), w.astype(np.float64)
    y = np.stack([sum(W[r][:, 128 * j:128 * j + 128].T @ X[j if r < NT else j + NT] for j in range(NT)) for r in range(N)])
    return {"y": y.astype(ml_dtypes.bfloat16 if x.dtype != np.float64 else np.float64)}

from concourse.bass import DstId, RemoteDMATransfer

P, TK = 128, 256
NT = 5

SCRATCH = {
    "xd": ("dram", [P, TK], "bfloat16"),
    "xs": ("sbuf", [P, NT * TK], "bfloat16"),
    "ws": ("sbuf", [P, NT * P], "bfloat16"),
    "ys": ("sbuf", [P, TK], "bfloat16"),
    "acc": ("psum", [P, TK], "float32"),
}
SEMAPHORES = ["t0", "t1", "t2", "t3", "t4", "ld", "lw", "hand", "sent", "mm", "cp", "st"]


def _bits(mask):
    return [b for b in range(mask.bit_length()) if (mask >> b) & 1]


def _count(mask):
    return len(_bits(mask))


def _plan(T, topo):
    cores = list(T.cores)
    nt = len(cores) // 2
    world = range((max(topo.host(c) for c in cores) + 1) * topo.CORES_PER_HOST)
    flows, used, load = [], set(), {}
    for s, src in enumerate(cores):
        for dst in cores:
            if dst == src or topo.host(dst) != topo.host(src):
                continue
            if topo.may_write(src, dst):
                flows.append((s % nt, src, None, dst))
                continue
            free = [c for c in world
                    if topo.host(c) == topo.host(src) and topo.chip(c) == topo.chip(src)
                    and T.rank_of(c) is None and c not in used and topo.may_write(c, dst)]
            via = min(free, key=lambda c: (load.get((dst, topo.die(c)), 0) + load.get((src, topo.die(c)), 0),
                                           topo.die(c) != topo.die(src), c))
            used.add(via)
            for end in (src, dst):
                load[(end, topo.die(via))] = load.get((end, topo.die(via)), 0) + 1
            flows.append((s % nt, src, via, dst))
    return flows


def _dst(topo, dst, src):
    rid, pid = topo.addr(dst, src)
    return DstId(rid=rid, pnc=pid)


def rank_program(g, core, T, topo):
    flows = _plan(T, topo)
    rank = T.rank_of(core)

    if rank is None:
        mine = [f for f in flows if f[2] == core]
        if not mine:
            return
        (j, src, _, dst), = mine
        direct = [f[3] for f in flows if f[1] == src and f[2] is None]
        handed = _count(topo.mask(src, core) & ~topo.mask(src, direct[0]))
        m = topo.mask(core, dst)
        rid, pid = topo.addr(dst, core)
        g.wait_ge(T.sem.hand, handed)
        g.remote_dma(T.xs[:, j * TK:(j + 1) * TK], T.xd[:], T.sem["t%d" % j], T.sem.sent, pid, rid, m)
        g.wait_ge(T.sem.sent, _count(m))
        return

    own = rank % NT
    tsem = [T.sem["t%d" % j] for j in range(NT)]
    slot = [T.xs[:, j * TK:(j + 1) * TK] for j in range(NT)]

    g.sync.dma_start(T.xd[:], T.x[:]).then_inc(T.sem.ld, 16)
    g.sync.dma_start(slot[own], T.x[:]).then_inc(tsem[own], 16)
    g.sync.dma_start(T.ws[:], T.w[:]).then_inc(T.sem.lw, 16)

    vias = [f[2] for f in flows if f[1] == core and f[2] is not None]
    direct = [f[3] for f in flows if f[1] == core and f[2] is None]
    m_off = topo.mask(core, direct[0])
    m_on = topo.mask(core, vias[0]) & ~m_off
    g.wait_ge(T.sem.ld, 16)
    g.remote_dma_fused([RemoteDMATransfer(dst_ids=[_dst(topo, v, core) for v in vias], dma_engine_mask=m_on,
                                          remote_sem=T.sem.hand, srcs=[T.xd[:]], dsts=[T.xd[:] for v in vias])],
                       local_sem=T.sem.sent)
    g.remote_dma_fused([RemoteDMATransfer(dst_ids=[_dst(topo, d, core) for d in direct], dma_engine_mask=m_off,
                                          remote_sem=tsem[own], srcs=[T.xd[:]], dsts=[slot[own] for d in direct])],
                       local_sem=T.sem.sent)

    inc = [f for f in flows if f[3] == core]
    order = [(own, 16)]
    order += [(f[0], _count(topo.mask(f[1], core))) for f in inc if f[2] is None]
    order += [(f[0], _count(topo.mask(f[2], core))) for f in inc if f[2] is not None]
    g.tensor.wait_ge(T.sem.lw, 16)
    for k, (j, need) in enumerate(order):
        g.tensor.wait_ge(tsem[j], need)
        mmul = g.tensor.matmul(T.acc[:], T.ws[:, j * P:(j + 1) * P], slot[j], k == 0, k == len(order) - 1)
    mmul.then_inc(T.sem.mm, 1)

    g.vector.wait_ge(T.sem.mm, 1)
    g.vector.tensor_copy(T.ys[:], T.acc[:]).then_inc(T.sem.cp, 1)
    g.sync.wait_ge(T.sem.cp, 1)
    g.sync.dma_start(T.y[:], T.ys[:]).then_inc(T.sem.st, 16)
    g.sync.wait_ge(T.sem.st, 16)
    g.wait_ge(T.sem.sent, _count(m_on) + _count(m_off))
